import numpy as np
import ml_dtypes


def mxq(x, axis, fmt="e4m3"):
    dtype, down = {"e4m3": (ml_dtypes.float8_e4m3fn, 7), "e5m2": (ml_dtypes.float8_e5m2, 14)}[fmt]
    v = np.moveaxis(np.asarray(x, np.float32).astype(ml_dtypes.bfloat16).astype(np.float64), axis, -1)
    blocks = v.reshape(v.shape[:-1] + (-1, 32))
    amax = np.abs(blocks).max(-1, keepdims=True)
    byte = np.maximum(np.where(amax > 0, np.frexp(amax)[1] - 1 + 127, 0) - down, 1)
    scale = np.exp2(byte - 127.0)
    codes = (blocks / scale).astype(np.float32).astype(dtype).astype(np.float64)
    return np.moveaxis((codes * scale).reshape(v.shape), -1, axis)


WIDE = False


def mx_kscale(k):
    if not WIDE:
        return np.ones(k)
    levels = np.array([10, -10, 5, -5, 0])
    if k % 512:
        return np.exp2(np.random.permutation(np.resize(levels, k // 32))).repeat(32)
    a = np.empty((k // 512, 16))
    for p in range(k // 512):
        a[p, :8] = np.random.permutation(np.resize(levels, 8))
        for g in range(8):
            far = levels[np.abs(levels - a[p, g]) >= 10]
            a[p, g + 8] = far[np.random.randint(len(far))]
    return np.exp2(a.ravel()).repeat(32)


def f64(x):
    return np.asarray(x).astype(np.float64)


def striped(idx):
    return np.tile(idx.reshape(-1, 16).T, (8, 1)).astype(np.uint16)


def unstriped(offs):
    return offs[:16].T.reshape(-1).astype(np.int64)


def striped8(idx):
    return np.concatenate([x.reshape(-1, 16).T for x in idx]).astype(np.uint16)


def runs(offs, k):
    lists = np.stack([offs[16 * r : 16 * r + 16].T.reshape(-1) for r in range(8)]).astype(np.int64)
    return lists[np.arange(k) % 512 // 64]


def pack_weight(w):
    k, n = w.shape
    w = f64(np.asarray(w, np.float32).astype(ml_dtypes.bfloat16)).reshape(k // 32, 32, n)
    amax = np.abs(w).max(1)
    byte = np.clip(np.where(amax > 0, np.frexp(amax)[1] - 1 + 127 - 7, 1), 1, 254)
    scaled = (w * np.exp2(127.0 - byte)[:, None, :]).reshape(k, n).astype(np.float32)
    words = np.ascontiguousarray(scaled.reshape(k // 512, 128, 4, n).transpose(0, 1, 3, 2)).astype(ml_dtypes.float8_e4m3fn).view(np.uint8)
    return words, np.ascontiguousarray(byte.astype(np.uint8).reshape(k // 512, 16, n))


def unpack_weight(words, scales):
    g, p, n, _ = words.shape
    vals = np.ascontiguousarray(words).view(ml_dtypes.float8_e4m3fn).astype(np.float64) * np.repeat(np.exp2(scales.astype(np.float64) - 127.0), 8, axis=1)[..., None]
    return vals.transpose(0, 1, 3, 2).reshape(g * 512, n)

def planes(y):
    n, m = y.shape
    v = y.astype(np.float32).astype(ml_dtypes.bfloat16).astype(np.float64).reshape(n // 32, 32, m)
    top = np.abs(v).max(1)
    byte = np.clip(np.where(top > 0, np.frexp(top)[1] - 1 + 127 - 7, 1), 1, 254)
    codes = (v * np.exp2(127.0 - byte)[:, None, :]).reshape(n, m).astype(np.float32).astype(ml_dtypes.float8_e4m3fn).view(np.uint8)
    words = codes.reshape(n // 512, 128, 4, m).transpose(0, 1, 3, 2)
    return np.ascontiguousarray(words), np.ascontiguousarray(byte.astype(np.uint8).reshape(n // 512, 16, m))


K, T, S, N, H = 512, 2048, 512, 512, 512


def setup_inputs():
    n = np.random.standard_normal
    s = mx_kscale(K)[:, None]
    u = mx_kscale(H)
    packed_xT = pack_weight(n((K, T)) * s)
    packed_w1 = pack_weight(n((K, H)) / np.sqrt(K) / s)
    packed_w2 = pack_weight(n((H, N)) / np.sqrt(H) / u[:, None])
    packed_w3 = pack_weight(n((K, N)) / np.sqrt(K) / s)
    return {
        "x_words": packed_xT[0],
        "x_scales": packed_xT[1],
        "w1_words": packed_w1[0],
        "w1_scales": packed_w1[1],
        "gn": (np.random.uniform(0.5, 1.5, (H, 1)) * u[:, None]).astype(np.float32),
        "w2_words": packed_w2[0],
        "w2_scales": packed_w2[1],
        "w3_words": packed_w3[0],
        "w3_scales": packed_w3[1],
        "offs": striped(np.random.permutation(T)[:S]),
        "n1": striped8(np.stack([np.random.permutation(S) for _ in range(8)])),
        "two": striped(np.random.permutation(T)[:S]),
        "n2": striped8(np.stack([np.random.permutation(S) for _ in range(8)])),
        "n3": striped8(np.stack([np.random.permutation(S) for _ in range(8)])),
    }


def reference(x_words, x_scales, w1_words, w1_scales, gn, w2_words, w2_scales, w3_words, w3_scales, offs, n1, two, n2, n3):
    xq = unpack_weight(x_words, x_scales)[:, unstriped(offs)]
    y = unpack_weight(w1_words, w1_scales).T @ xq
    z = f64(gn) * (np.maximum(y, y[np.arange(H)[:, None], runs(n1, H)]))
    h = unpack_weight(w2_words, w2_scales).T @ mxq(z, 0, "e4m3")
    x_two = unpack_weight(x_words, x_scales)[:, unstriped(two)]
    d = unpack_weight(w3_words, w3_scales).T @ x_two
    out_0 = 0.75 * (h * (d[np.arange(N)[:, None], runs(n3, N)]) - ((h[np.arange(N)[:, None], runs(n2, N)]) * d))
    return (out_0,) + planes(out_0)

@@ -1,0 +1,190 @@
+from contextlib import ExitStack
+
+import concourse.mybir as mybir
+
+F32 = mybir.dt.float32
+BF16 = mybir.dt.bfloat16
+I32 = mybir.dt.int32
+U32 = mybir.dt.uint32
+U16 = mybir.dt.uint16
+U8 = mybir.dt.uint8
+FP8X4 = mybir.dt.float8_e4m3fn_x4
+COPY = mybir.ActivationFunctionType.Copy
+MULT = mybir.AluOpType.mult
+MAX = mybir.AluOpType.max
+SUB = mybir.AluOpType.subtract
+
+P = 128
+T = 2048
+S = 512
+HALF = S // 2
+FLOPS = 3 * 2 * 512 * 512 * 512
+V_COLS = 176
+
+
+def tile_picked_latecrossbbig_none_po_kernel(
+    tc, x_words, x_scales, w1_words, w1_scales, gn, w2_words, w2_scales, w3_words, w3_scales,
+    offs, n1, two, n2, n3, out_0, out_1, out_2,
+):
+    nc = tc.nc
+    with ExitStack() as ctx:
+        keep = ctx.enter_context(tc.tile_pool(name="keep", bufs=1))
+        psum = ctx.enter_context(tc.psum_pool(name="psum", bufs=1))
+
+        def load_list(name, src):
+            tile = keep.tile([P, S // 16], U16, name=name)
+            nc.sync.dma_start(tile[:], src)
+            return tile
+
+        def load_words(name, src, width):
+            tile = keep.tile([P, width], I32, name=name, align_bytes=64)
+            nc.sync.dma_start(tile[:], src[0].rearrange("p n r -> p (n r)").bitcast(I32))
+            return tile
+
+        def load_scale_rows(tile, src, first):
+            for q in range(4):
+                nc.sync.dma_start(
+                    tile[32 * q + first : 32 * q + first + 4, :].bitcast(I32),
+                    src[0, 4 * q : 4 * q + 4, :].bitcast(I32),
+                )
+
+        def deal(name, raw, dtype):
+            dealt = keep.tile([P, S], dtype, name=name, align_bytes=64)
+            nc.vector.tensor_copy(
+                dealt[:].rearrange("p (t m) -> p m t", t=4), raw[:].rearrange("p (m t) -> p m t", t=4)
+            )
+            return dealt
+
+        def half_cols(a):
+            return slice(a * HALF, (a + 1) * HALF)
+
+        def half_list(tile, a):
+            return tile[:, a * (HALF // 16) : (a + 1) * (HALF // 16)]
+
+        xs = keep.tile([P, T], U8, name="xs", align_bytes=64)
+        nc.vector.memset(xs[:].bitcast(I32), 0)
+        ws1_raw = keep.tile([P, S], U8, name="ws1_raw", tag="ws1_then_xw_two", align_bytes=64)
+        ws32_raw = keep.tile([P, S], U8, name="ws32_raw", align_bytes=64)
+        nc.vector.memset(ws1_raw[:].bitcast(I32), 0)
+        nc.gpsimd.memset(ws32_raw[:].bitcast(I32), 0)
+
+        offs_sb = load_list("offs_sb", offs)
+        load_scale_rows(xs, x_scales, 0)
+        two_sb = load_list("two_sb", two)
+        xw = load_words("xw", x_words, T)
+        w1_raw = load_words("w1_raw", w1_words, S)
+        load_scale_rows(ws1_raw, w1_scales, 0)
+        n1_sb = load_list("n1_sb", n1)
+        gn_sb = keep.tile([P, 4], F32, name="gn_sb")
+        nc.sync.dma_start(gn_sb[:], gn.rearrange("(p t) o -> p (t o)", t=4))
+        w3_raw = load_words("w3_raw", w3_words, S)
+        load_scale_rows(ws32_raw, w3_scales, 0)
+        load_scale_rows(ws32_raw, w2_scales, 4)
+        w2_raw = load_words("w2_raw", w2_words, S)
+        n3_sb = load_list("n3_sb", n3)
+        n2_sb = load_list("n2_sb", n2)
+
+        def pick_scales(name, lst):
+            tile = keep.tile([P, S], U8, name=name, align_bytes=64)
+            nc.vector.tensor_copy(tile[:], xs[:].indirect(lst[:]))
+            return tile
+
+        def pick_words(name, lst, tag):
+            tile = keep.tile([P, S], U32, name=name, tag=tag, align_bytes=64)
+            nc.vector.tensor_copy(tile[:], xw[:].bitcast(U32).indirect(lst[:]))
+            return tile
+
+        def product(bank, width, words, scales, first, t, rhs_words, rhs_scales):
+            acc = psum.tile([P, width], F32, name="acc", tag="bank%d" % bank)
+            cols = slice(P * t, P * (t + 1))
+            nc.tensor.matmul_mx(
+                out=acc[:], lhsT=words[:, cols].bitcast(FP8X4), lhsT_scale=scales[first:P, cols],
+                rhs=rhs_words[:].bitcast(FP8X4), rhs_scale=rhs_scales[:], start=True, stop=True,
+            )
+            return acc
+
+        xs_one = pick_scales("xs_one", offs_sb)
+        xs_two = pick_scales("xs_two", two_sb)
+        xw_one = pick_words("xw_one", offs_sb, "xw_one")
+        w1 = deal("w1", w1_raw, I32)
+        ws1 = deal("ws1", ws1_raw, U8)
+        xw_two = pick_words("xw_two", two_sb, "ws1_then_xw_two")
+
+        y = []
+        for t in range(4):
+            acc = product(t, S, w1, ws1, 0, t, xw_one, xs_one)
+            y_t = keep.tile([P, S], F32, name="y%d" % t)
+            nc.scalar.activation(y_t[:], acc[:], COPY)
+            y.append(y_t)
+
+        w3 = deal("w3", w3_raw, I32)
+        ws32 = deal("ws32", ws32_raw, U8)
+
+        planes = [keep.tile([P, 4, HALF], BF16, name="planes%d" % a) for a in range(2)]
+        d = []
+        for t in range(4):
+            fetched = keep.tile([P, S], F32, name="yn%d" % t)
+            larger = keep.tile([P, S], F32, name="larger%d" % t)
+            for a in range(2):
+                nc.vector.tensor_copy(fetched[:, half_cols(a)], y[t][:].indirect(half_list(n1_sb, a)))
+            pieces = [slice(0, S)] if t < 3 else [half_cols(0), half_cols(1)]
+            for cols in pieces:
+                nc.vector.tensor_tensor(larger[:, cols], fetched[:, cols], y[t][:, cols], MAX)
+            for a in range(2):
+                nc.scalar.activation(planes[a][:, t, :], larger[:, half_cols(a)], COPY, scale=gn_sb[:, t : t + 1])
+            acc = product(4 + t, S, w3, ws32, 0, t, xw_two, xs_two)
+            d_t = keep.tile([P, S], F32, name="d%d" % t)
+            nc.scalar.activation(d_t[:], acc[:], COPY, scale=0.75)
+            d.append(d_t)
+
+        woven = [keep.tile([P, HALF, 4], BF16, name="woven%d" % a, align_bytes=64) for a in range(2)]
+        nc.vector.tensor_copy(woven[0][:], planes[0][:].rearrange("p t j -> p j t"))
+        nc.scalar.copy(woven[1][:], planes[1][:].rearrange("p t j -> p j t"))
+        w2 = deal("w2", w2_raw, I32)
+
+        h = [keep.tile([P, S], F32, name="h%d" % t) for t in range(4)]
+        h_acc = []
+        for a in range(2):
+            zw = keep.tile([P, HALF], U32, name="zw%d" % a, align_bytes=64)
+            zs = keep.tile([P, HALF], U8, name="zs%d" % a, align_bytes=64)
+            nc.vector.quantize_mx(out=zw[:].bitcast(FP8X4), scales=zs[:], in_=woven[a][:].rearrange("p j t -> p (j t)"))
+            for t in range(4):
+                h_acc.append(product(4 * a + t, HALF, w2, ws32, 4, t, zw, zs))
+                if a == 0:
+                    nc.scalar.activation(h[t][:, half_cols(0)], h_acc[t][:], COPY)
+
+        out_scales = keep.tile([P, S], U8, name="out_scales", align_bytes=64)
+        out_rows = out_0.rearrange("(p t) j -> p t j", t=4)
+        out_words = out_1[0].rearrange("p n r -> p (n r)").bitcast(I32)
+        for a in range(2):
+            cols = half_cols(a)
+            left = keep.tile([P, 4, HALF], F32, name="left%d" % a)
+            right = keep.tile([P, 4, HALF], F32, name="right%d" % a)
+            res = keep.tile([P, 4, HALF], F32, name="res%d" % a)
+            for t in range(4):
+                nc.vector.tensor_tensor(left[:, t, :], d[t][:].indirect(half_list(n3_sb, a)), h[t][:, cols], MULT)
+                if a == 0:
+                    nc.scalar.activation(h[t][:, half_cols(1)], h_acc[4 + t][:], COPY)
+            groups = [(0, 2), (2, 4)] if a == 0 else [(0, 2), (2, 3), (3, 4)]
+            for t in range(4):
+                nc.vector.tensor_tensor(right[:, t, :], h[t][:].indirect(half_list(n2_sb, a)), d[t][:, cols], MULT)
+            for lo, hi in groups:
+                nc.vector.tensor_tensor(res[:, lo:hi, :], left[:, lo:hi, :], right[:, lo:hi, :], SUB)
+                nc.sync.dma_start(out_rows[:, lo:hi, cols], res[:, lo:hi, :])
+            rounded = keep.tile([P, HALF, 4], BF16, name="rounded%d" % a, align_bytes=64)
+            by_col = res[:].rearrange("p t j -> p j t")
+            if a == 0:
+                nc.scalar.copy(rounded[:], by_col)
+            else:
+                nc.scalar.copy(rounded[:, V_COLS:, :], by_col[:, V_COLS:, :])
+                nc.vector.tensor_copy(rounded[:, :V_COLS, :], by_col[:, :V_COLS, :])
+            codes = keep.tile([P, HALF], I32, name="codes%d" % a, align_bytes=64)
+            nc.vector.quantize_mx(
+                out=codes[:].bitcast(FP8X4), scales=out_scales[:, cols], in_=rounded[:].rearrange("p j t -> p (j t)")
+            )
+            nc.sync.dma_start(out_words[:, cols], codes[:])
+        for q in range(4):
+            queue = nc.scalar if q % 2 == 0 else nc.sync
+            queue.dma_start(
+                out_2[0, 4 * q : 4 * q + 4, :].bitcast(I32), out_scales[32 * q : 32 * q + 4, :].bitcast(I32)
+            )

@@ -1,6 +1,7 @@
 from contextlib import ExitStack
 
 import concourse.mybir as mybir
+from concourse.masks import make_identity
 
 F32 = mybir.dt.float32
 BF16 = mybir.dt.bfloat16
@@ -41,15 +42,15 @@ def tile_picked_latecrossbbig_none_po_kernel(
             nc.sync.dma_start(tile[:], src[0].rearrange("p n r -> p (n r)").bitcast(I32))
             return tile
 
-        def load_scale_rows(tile, src, first):
-            for q in range(4):
+        def load_scale_rows(tile, src, first, quadrants=range(4)):
+            for q in quadrants:
                 nc.sync.dma_start(
                     tile[32 * q + first : 32 * q + first + 4, :].bitcast(I32),
                     src[0, 4 * q : 4 * q + 4, :].bitcast(I32),
                 )
 
-        def deal(name, raw, dtype):
-            dealt = keep.tile([P, S], dtype, name=name, align_bytes=64)
+        def deal(name, raw, dtype, tag=""):
+            dealt = keep.tile([P, S], dtype, name=name, tag=tag or name, align_bytes=64)
             nc.vector.tensor_copy(
                 dealt[:].rearrange("p (t m) -> p m t", t=4), raw[:].rearrange("p (m t) -> p m t", t=4)
             )
@@ -64,9 +65,12 @@ def tile_picked_latecrossbbig_none_po_kernel(
         xs = keep.tile([P, T], U8, name="xs", align_bytes=64)
         nc.vector.memset(xs[:].bitcast(I32), 0)
         ws1_raw = keep.tile([P, S], U8, name="ws1_raw", tag="ws1_then_xw_two", align_bytes=64)
-        ws32_raw = keep.tile([P, S], U8, name="ws32_raw", align_bytes=64)
+        ws32_raw = keep.tile([P, S], U8, name="ws32_raw", tag="ws32_then_yn", align_bytes=64)
         nc.vector.memset(ws1_raw[:].bitcast(I32), 0)
-        nc.gpsimd.memset(ws32_raw[:].bitcast(I32), 0)
+        nc.vector.memset(ws32_raw[:].bitcast(I32), 0)
+
+        ident = keep.tile([P, P], F32, name="ident")
+        make_identity(nc, ident[:])
 
         offs_sb = load_list("offs_sb", offs)
         load_scale_rows(xs, x_scales, 0)
@@ -74,12 +78,13 @@ def tile_picked_latecrossbbig_none_po_kernel(
         xw = load_words("xw", x_words, T)
         w1_raw = load_words("w1_raw", w1_words, S)
         load_scale_rows(ws1_raw, w1_scales, 0)
+        w3_raw = load_words("w3_raw", w3_words, S)
+        load_scale_rows(ws32_raw, w3_scales, 0, range(0, 2))
         n1_sb = load_list("n1_sb", n1)
+        load_scale_rows(ws32_raw, w3_scales, 0, range(2, 4))
+        load_scale_rows(ws32_raw, w2_scales, 4)
         gn_sb = keep.tile([P, 4], F32, name="gn_sb")
         nc.sync.dma_start(gn_sb[:], gn.rearrange("(p t) o -> p (t o)", t=4))
-        w3_raw = load_words("w3_raw", w3_words, S)
-        load_scale_rows(ws32_raw, w3_scales, 0)
-        load_scale_rows(ws32_raw, w2_scales, 4)
         w2_raw = load_words("w2_raw", w2_words, S)
         n3_sb = load_list("n3_sb", n3)
         n2_sb = load_list("n2_sb", n2)
@@ -94,14 +99,15 @@ def tile_picked_latecrossbbig_none_po_kernel(
             nc.vector.tensor_copy(tile[:], xw[:].bitcast(U32).indirect(lst[:]))
             return tile
 
-        def product(bank, width, words, scales, first, t, rhs_words, rhs_scales):
-            acc = psum.tile([P, width], F32, name="acc", tag="bank%d" % bank)
+        def bank(index):
+            return psum.tile([P, S], F32, name="acc", tag="bank%d" % index)
+
+        def product(acc, words, scales, first, t, rhs_words, rhs_scales):
             cols = slice(P * t, P * (t + 1))
             nc.tensor.matmul_mx(
-                out=acc[:], lhsT=words[:, cols].bitcast(FP8X4), lhsT_scale=scales[first:P, cols],
+                out=acc, lhsT=words[:, cols].bitcast(FP8X4), lhsT_scale=scales[first:P, cols],
                 rhs=rhs_words[:].bitcast(FP8X4), rhs_scale=rhs_scales[:], start=True, stop=True,
             )
-            return acc
 
         xs_one = pick_scales("xs_one", offs_sb)
         xs_two = pick_scales("xs_two", two_sb)
@@ -112,7 +118,8 @@ def tile_picked_latecrossbbig_none_po_kernel(
 
         y = []
         for t in range(4):
-            acc = product(t, S, w1, ws1, 0, t, xw_one, xs_one)
+            acc = bank(t)
+            product(acc[:], w1, ws1, 0, t, xw_one, xs_one)
             y_t = keep.tile([P, S], F32, name="y%d" % t)
             nc.scalar.activation(y_t[:], acc[:], COPY)
             y.append(y_t)
@@ -121,68 +128,123 @@ def tile_picked_latecrossbbig_none_po_kernel(
         ws32 = deal("ws32", ws32_raw, U8)
 
         planes = [keep.tile([P, 4, HALF], BF16, name="planes%d" % a) for a in range(2)]
-        d = []
-        for t in range(4):
-            fetched = keep.tile([P, S], F32, name="yn%d" % t)
-            larger = keep.tile([P, S], F32, name="larger%d" % t)
-            for a in range(2):
-                nc.vector.tensor_copy(fetched[:, half_cols(a)], y[t][:].indirect(half_list(n1_sb, a)))
-            pieces = [slice(0, S)] if t < 3 else [half_cols(0), half_cols(1)]
-            for cols in pieces:
-                nc.vector.tensor_tensor(larger[:, cols], fetched[:, cols], y[t][:, cols], MAX)
-            for a in range(2):
-                nc.scalar.activation(planes[a][:, t, :], larger[:, half_cols(a)], COPY, scale=gn_sb[:, t : t + 1])
-            acc = product(4 + t, S, w3, ws32, 0, t, xw_two, xs_two)
-            d_t = keep.tile([P, S], F32, name="d%d" % t)
-            nc.scalar.activation(d_t[:], acc[:], COPY, scale=0.75)
-            d.append(d_t)
-
-        woven = [keep.tile([P, HALF, 4], BF16, name="woven%d" % a, align_bytes=64) for a in range(2)]
-        nc.vector.tensor_copy(woven[0][:], planes[0][:].rearrange("p t j -> p j t"))
-        nc.scalar.copy(woven[1][:], planes[1][:].rearrange("p t j -> p j t"))
-        w2 = deal("w2", w2_raw, I32)
-
+        woven = [keep.tile([P, HALF, 4], BF16, name="woven%d" % a, tag="woven%d" % a, align_bytes=64) for a in range(2)]
+        larger = [keep.tile([P, 4, HALF], F32, name="larger%d" % a, tag="larger%d" % a, align_bytes=64) for a in range(2)]
+        d = [keep.tile([P, S], F32, name="d%d" % t) for t in range(4)]
         h = [keep.tile([P, S], F32, name="h%d" % t) for t in range(4)]
-        h_acc = []
-        for a in range(2):
+        h_neg = [keep.tile([P, HALF], F32, name="h_neg%d" % t) for t in range(4)]
+
+        def fetch(dst, t, a):
+            nc.vector.tensor_copy(dst, y[t][:].indirect(half_list(n1_sb, a)))
+
+        def larger_scaled(fetched, t, a):
+            nc.vector.tensor_tensor(larger[a][:, t, :], fetched, y[t][:, half_cols(a)], MAX)
+            nc.scalar.activation(planes[a][:, t, :], larger[a][:, t, :], COPY, scale=gn_sb[:, t : t + 1])
+
+        def weave_z(a):
+            nc.scalar.copy(woven[a][:], planes[a][:].rearrange("p t j -> p j t"))
+
+        def h_products(a):
             zw = keep.tile([P, HALF], U32, name="zw%d" % a, align_bytes=64)
             zs = keep.tile([P, HALF], U8, name="zs%d" % a, align_bytes=64)
             nc.vector.quantize_mx(out=zw[:].bitcast(FP8X4), scales=zs[:], in_=woven[a][:].rearrange("p j t -> p (j t)"))
             for t in range(4):
-                h_acc.append(product(4 * a + t, HALF, w2, ws32, 4, t, zw, zs))
-                if a == 0:
-                    nc.scalar.activation(h[t][:, half_cols(0)], h_acc[t][:], COPY)
+                product(h_acc[t][:, half_cols(a)], w2, ws32, 4, t, zw, zs)
+
+        yn_first = keep.tile([P, HALF], F32, name="yn_first")
+        yn_ring = keep.tile([P, 3, HALF], F32, name="yn_ring", tag="ws32_then_yn", align_bytes=64)
+        pieces = [(t, 0) for t in range(4)] + [(0, 1), (1, 1)]
+        before = None
+        for i, (t, a) in enumerate(pieces):
+            yn = yn_first[:] if i == 0 else yn_ring[:, i % 3, :]
+            fetch(yn, t, a)
+            if a == 0:
+                acc = bank(4 + t)
+                product(acc[:], w3, ws32, 0, t, xw_two, xs_two)
+                nc.scalar.activation(d[t][:], acc[:], COPY, scale=0.75)
+            if before is not None:
+                larger_scaled(*before)
+                if before[1:] == (3, 0):
+                    weave_z(0)
+            before = (yn, t, a)
+        larger_scaled(*before)
+        w2 = deal("w2", w2_raw, I32, "larger0")
+        h_acc = [bank(t) for t in range(4)]
+        h_products(0)
+        for t in range(4):
+            nc.scalar.activation(h_neg[t][:], h_acc[t][:, half_cols(0)], COPY, scale=-1.0)
+        yn_late = keep.tile([P, 2, HALF], F32, name="yn_late", tag="woven0", align_bytes=64)
+        for t in range(2, 4):
+            fetch(yn_late[:, t - 2, :], t, 1)
+        for t in range(2, 4):
+            larger_scaled(yn_late[:, t - 2, :], t, 1)
+        weave_z(1)
 
         out_scales = keep.tile([P, S], U8, name="out_scales", align_bytes=64)
         out_rows = out_0.rearrange("(p t) j -> p t j", t=4)
         out_words = out_1[0].rearrange("p n r -> p (n r)").bitcast(I32)
-        for a in range(2):
-            cols = half_cols(a)
-            left = keep.tile([P, 4, HALF], F32, name="left%d" % a)
-            right = keep.tile([P, 4, HALF], F32, name="right%d" % a)
-            res = keep.tile([P, 4, HALF], F32, name="res%d" % a)
-            for t in range(4):
-                nc.vector.tensor_tensor(left[:, t, :], d[t][:].indirect(half_list(n3_sb, a)), h[t][:, cols], MULT)
-                if a == 0:
-                    nc.scalar.activation(h[t][:, half_cols(1)], h_acc[4 + t][:], COPY)
-            groups = [(0, 2), (2, 4)] if a == 0 else [(0, 2), (2, 3), (3, 4)]
-            for t in range(4):
-                nc.vector.tensor_tensor(right[:, t, :], h[t][:].indirect(half_list(n2_sb, a)), d[t][:, cols], MULT)
-            for lo, hi in groups:
-                nc.vector.tensor_tensor(res[:, lo:hi, :], left[:, lo:hi, :], right[:, lo:hi, :], SUB)
-                nc.sync.dma_start(out_rows[:, lo:hi, cols], res[:, lo:hi, :])
-            rounded = keep.tile([P, HALF, 4], BF16, name="rounded%d" % a, align_bytes=64)
-            by_col = res[:].rearrange("p t j -> p j t")
-            if a == 0:
-                nc.scalar.copy(rounded[:], by_col)
-            else:
-                nc.scalar.copy(rounded[:, V_COLS:, :], by_col[:, V_COLS:, :])
-                nc.vector.tensor_copy(rounded[:, :V_COLS, :], by_col[:, :V_COLS, :])
+        left_second = keep.tile([P, 4, HALF], F32, name="left_second")
+        right = [keep.tile([P, 4, HALF], F32, name="right%d" % a) for a in range(2)]
+        res = [keep.tile([P, 4, HALF], F32, name="res%d" % a) for a in range(2)]
+        rounded = [keep.tile([P, HALF, 4], BF16, name="rounded%d" % a, align_bytes=64) for a in range(2)]
+
+        def left_product(dst, a, t, plain):
+            nc.vector.tensor_tensor(dst, d[t][:].indirect(half_list(n3_sb, a)), plain, MULT)
+
+        def right_product(a, t):
+            nc.vector.tensor_tensor(right[a][:, t, :], h[t][:].indirect(half_list(n2_sb, a)), d[t][:, half_cols(a)], MULT)
+
+        def quantise_result(a):
             codes = keep.tile([P, HALF], I32, name="codes%d" % a, align_bytes=64)
             nc.vector.quantize_mx(
-                out=codes[:].bitcast(FP8X4), scales=out_scales[:, cols], in_=rounded[:].rearrange("p j t -> p (j t)")
+                out=codes[:].bitcast(FP8X4), scales=out_scales[:, half_cols(a)],
+                in_=rounded[a][:].rearrange("p j t -> p (j t)"),
             )
-            nc.sync.dma_start(out_words[:, cols], codes[:])
+            nc.sync.dma_start(out_words[:, half_cols(a)], codes[:])
+
+        left_early = keep.tile([P, 3, HALF], F32, name="left_early")
+        for t in range(3):
+            left_product(left_early[:, t, :], 0, t, h_neg[t][:])
+        h_products(1)
+        left_late = keep.tile([P, HALF], F32, name="left_late", tag="woven1", align_bytes=64)
+        left_product(left_late[:], 0, 3, h_neg[3][:])
+        left_first = [left_early[:, 0, :], left_early[:, 1, :], left_early[:, 2, :], left_late[:]]
+        for t in range(4):
+            nc.scalar.activation(h[t][:], h_acc[t][:], COPY)
+        for pair in range(2):
+            turned = bank(4 + pair)
+            for u in range(2):
+                t = 2 * pair + u
+                right_product(0, t)
+                for b in range(2):
+                    blk = slice(P * b, P * (b + 1))
+                    dst = turned[:, HALF * u + P * b : HALF * u + P * (b + 1)]
+                    nc.tensor.matmul(dst, left_first[t][:, blk], ident[:], start=True, stop=False, is_transpose=True)
+                    nc.tensor.matmul(dst, right[0][:, t, blk], ident[:], start=False, stop=True, is_transpose=True)
+            turned_sb = keep.tile([P, S], F32, name="turned_sb%d" % pair)
+            nc.scalar.activation(turned_sb[:], turned[:], COPY, scale=-1.0)
+            back = bank(6 + pair)
+            for b in range(4):
+                blk = slice(P * b, P * (b + 1))
+                nc.tensor.transpose(back[:, blk], turned_sb[:, blk], ident[:])
+            rows = slice(2 * pair, 2 * pair + 2)
+            nc.scalar.activation(res[0][:, rows, :].rearrange("p t j -> p (t j)"), back[:], COPY)
+            nc.sync.dma_start(out_rows[:, rows, half_cols(0)], res[0][:, rows, :])
+        nc.scalar.copy(rounded[0][:], res[0][:].rearrange("p t j -> p j t"))
+
+        for t in range(4):
+            left_product(left_second[:, t, :], 1, t, h[t][:, half_cols(1)])
+        for t in range(4):
+            right_product(1, t)
+            if t == 1:
+                quantise_result(0)
+        for lo, hi in [(0, 2), (2, 3), (3, 4)]:
+            nc.vector.tensor_tensor(res[1][:, lo:hi, :], left_second[:, lo:hi, :], right[1][:, lo:hi, :], SUB)
+            nc.sync.dma_start(out_rows[:, lo:hi, half_cols(1)], res[1][:, lo:hi, :])
+        by_col = res[1][:].rearrange("p t j -> p j t")
+        nc.scalar.copy(rounded[1][:, V_COLS:, :], by_col[:, V_COLS:, :])
+        nc.vector.tensor_copy(rounded[1][:, :V_COLS, :], by_col[:, :V_COLS, :])
+        quantise_result(1)
         for q in range(4):
             queue = nc.scalar if q % 2 == 0 else nc.sync
             queue.dma_start(

@@ -19,8 +19,9 @@ P = 128
 T = 2048
 S = 512
 HALF = S // 2
-FLOPS = 3 * 2 * 512 * 512 * 512
+ROW_GROUPS = ((0, 2), (2, 3), (3, 4))
 V_COLS = 176
+FLOPS = 3 * 2 * 512 * 512 * 512
 
 
 def tile_picked_latecrossbbig_none_po_kernel(
@@ -42,8 +43,8 @@ def tile_picked_latecrossbbig_none_po_kernel(
             nc.sync.dma_start(tile[:], src[0].rearrange("p n r -> p (n r)").bitcast(I32))
             return tile
 
-        def load_scale_rows(tile, src, first, quadrants=range(4)):
-            for q in quadrants:
+        def load_scale_rows(tile, src, first):
+            for q in range(4):
                 nc.sync.dma_start(
                     tile[32 * q + first : 32 * q + first + 4, :].bitcast(I32),
                     src[0, 4 * q : 4 * q + 4, :].bitcast(I32),
@@ -51,10 +52,15 @@ def tile_picked_latecrossbbig_none_po_kernel(
 
         def deal(name, raw, dtype, tag=""):
             dealt = keep.tile([P, S], dtype, name=name, tag=tag or name, align_bytes=64)
+            run = 4 if dtype == I32 else P
             nc.vector.tensor_copy(
-                dealt[:].rearrange("p (t m) -> p m t", t=4), raw[:].rearrange("p (m t) -> p m t", t=4)
+                dealt[:].rearrange("p (t c i) -> p c t i", t=4, i=run),
+                raw[:].rearrange("p (c i t) -> p c t i", t=4, i=run),
             )
             return dealt
+
+        def weave(copy, dst, src):
+            copy(dst.rearrange("p (c i) t -> p c t i", i=4), src.rearrange("p t (c i) -> p c t i", i=4))
 
         def half_cols(a):
             return slice(a * HALF, (a + 1) * HALF)
@@ -64,8 +70,8 @@ def tile_picked_latecrossbbig_none_po_kernel(
 
         xs = keep.tile([P, T], U8, name="xs", align_bytes=64)
         nc.vector.memset(xs[:].bitcast(I32), 0)
-        ws1_raw = keep.tile([P, S], U8, name="ws1_raw", tag="ws1_then_xw_two", align_bytes=64)
-        ws32_raw = keep.tile([P, S], U8, name="ws32_raw", tag="ws32_then_yn", align_bytes=64)
+        ws1_raw = keep.tile([P, S], U8, name="ws1_raw", align_bytes=64)
+        ws32_raw = keep.tile([P, S], U8, name="ws32_raw", align_bytes=64)
         nc.vector.memset(ws1_raw[:].bitcast(I32), 0)
         nc.vector.memset(ws32_raw[:].bitcast(I32), 0)
 
@@ -76,13 +82,12 @@ def tile_picked_latecrossbbig_none_po_kernel(
         load_scale_rows(xs, x_scales, 0)
         two_sb = load_list("two_sb", two)
         xw = load_words("xw", x_words, T)
-        w1_raw = load_words("w1_raw", w1_words, S)
         load_scale_rows(ws1_raw, w1_scales, 0)
+        w1_raw = load_words("w1_raw", w1_words, S)
         w3_raw = load_words("w3_raw", w3_words, S)
-        load_scale_rows(ws32_raw, w3_scales, 0, range(0, 2))
-        n1_sb = load_list("n1_sb", n1)
-        load_scale_rows(ws32_raw, w3_scales, 0, range(2, 4))
+        load_scale_rows(ws32_raw, w3_scales, 0)
         load_scale_rows(ws32_raw, w2_scales, 4)
+        n1_sb = load_list("n1_sb", n1)
         gn_sb = keep.tile([P, 4], F32, name="gn_sb")
         nc.sync.dma_start(gn_sb[:], gn.rearrange("(p t) o -> p (t o)", t=4))
         w2_raw = load_words("w2_raw", w2_words, S)
@@ -112,9 +117,8 @@ def tile_picked_latecrossbbig_none_po_kernel(
         xs_one = pick_scales("xs_one", offs_sb)
         xs_two = pick_scales("xs_two", two_sb)
         xw_one = pick_words("xw_one", offs_sb, "xw_one")
-        w1 = deal("w1", w1_raw, I32)
         ws1 = deal("ws1", ws1_raw, U8)
-        xw_two = pick_words("xw_two", two_sb, "ws1_then_xw_two")
+        w1 = deal("w1", w1_raw, I32)
 
         y = []
         for t in range(4):
@@ -125,11 +129,12 @@ def tile_picked_latecrossbbig_none_po_kernel(
             y.append(y_t)
 
         w3 = deal("w3", w3_raw, I32)
+        xw_two = pick_words("xw_two", two_sb, "w1_raw")
         ws32 = deal("ws32", ws32_raw, U8)
 
-        planes = [keep.tile([P, 4, HALF], BF16, name="planes%d" % a) for a in range(2)]
-        woven = [keep.tile([P, HALF, 4], BF16, name="woven%d" % a, tag="woven%d" % a, align_bytes=64) for a in range(2)]
-        larger = [keep.tile([P, 4, HALF], F32, name="larger%d" % a, tag="larger%d" % a, align_bytes=64) for a in range(2)]
+        planes = [keep.tile([P, 4, HALF], BF16, name="planes%d" % a, tag="planes%d" % a, align_bytes=64) for a in range(2)]
+        woven = [keep.tile([P, HALF, 4], BF16, name="woven%d" % a, align_bytes=64) for a in range(2)]
+        larger = [keep.tile([P, 4, HALF], F32, name="larger%d" % a) for a in range(2)]
         d = [keep.tile([P, S], F32, name="d%d" % t) for t in range(4)]
         h = [keep.tile([P, S], F32, name="h%d" % t) for t in range(4)]
         h_neg = [keep.tile([P, HALF], F32, name="h_neg%d" % t) for t in range(4)]
@@ -142,7 +147,7 @@ def tile_picked_latecrossbbig_none_po_kernel(
             nc.scalar.activation(planes[a][:, t, :], larger[a][:, t, :], COPY, scale=gn_sb[:, t : t + 1])
 
         def weave_z(a):
-            nc.scalar.copy(woven[a][:], planes[a][:].rearrange("p t j -> p j t"))
+            weave(nc.scalar.copy, woven[a][:], planes[a][:])
 
         def h_products(a):
             zw = keep.tile([P, HALF], U32, name="zw%d" % a, align_bytes=64)
@@ -151,48 +156,53 @@ def tile_picked_latecrossbbig_none_po_kernel(
             for t in range(4):
                 product(h_acc[t][:, half_cols(a)], w2, ws32, 4, t, zw, zs)
 
-        yn_first = keep.tile([P, HALF], F32, name="yn_first")
-        yn_ring = keep.tile([P, 3, HALF], F32, name="yn_ring", tag="ws32_then_yn", align_bytes=64)
-        pieces = [(t, 0) for t in range(4)] + [(0, 1), (1, 1)]
-        before = None
-        for i, (t, a) in enumerate(pieces):
-            yn = yn_first[:] if i == 0 else yn_ring[:, i % 3, :]
-            fetch(yn, t, a)
-            if a == 0:
-                acc = bank(4 + t)
-                product(acc[:], w3, ws32, 0, t, xw_two, xs_two)
-                nc.scalar.activation(d[t][:], acc[:], COPY, scale=0.75)
-            if before is not None:
-                larger_scaled(*before)
-                if before[1:] == (3, 0):
-                    weave_z(0)
-            before = (yn, t, a)
-        larger_scaled(*before)
-        w2 = deal("w2", w2_raw, I32, "larger0")
+        def d_product(t):
+            acc = bank(4 + t)
+            product(acc[:], w3, ws32, 0, t, xw_two, xs_two)
+            nc.scalar.activation(d[t][:], acc[:], COPY, scale=0.75)
+
+        def negated_h(t):
+            nc.scalar.activation(h_neg[t][:], h_acc[t][:, half_cols(0)], COPY, scale=-1.0)
+
+        for t in range(3):
+            d_product(t)
+        yn_first = keep.tile([P, 4, HALF], F32, name="yn_first")
+        for t in range(4):
+            fetch(yn_first[:, t, :], t, 0)
+        for t in range(4):
+            larger_scaled(yn_first[:, t, :], t, 0)
+        d_product(3)
+        weave_z(0)
+        yn_early = keep.tile([P, 2, HALF], F32, name="yn_early")
+        for t in range(2):
+            fetch(yn_early[:, t, :], t, 1)
+        for t in range(2):
+            larger_scaled(yn_early[:, t, :], t, 1)
+        w2 = deal("w2", w2_raw, I32)
         h_acc = [bank(t) for t in range(4)]
         h_products(0)
-        for t in range(4):
-            nc.scalar.activation(h_neg[t][:], h_acc[t][:, half_cols(0)], COPY, scale=-1.0)
-        yn_late = keep.tile([P, 2, HALF], F32, name="yn_late", tag="woven0", align_bytes=64)
+        for t in range(3):
+            negated_h(t)
+        yn_late = keep.tile([P, 2, HALF], F32, name="yn_late", tag="planes0", align_bytes=64)
         for t in range(2, 4):
             fetch(yn_late[:, t - 2, :], t, 1)
         for t in range(2, 4):
             larger_scaled(yn_late[:, t - 2, :], t, 1)
+        negated_h(3)
         weave_z(1)
 
         out_scales = keep.tile([P, S], U8, name="out_scales", align_bytes=64)
         out_rows = out_0.rearrange("(p t) j -> p t j", t=4)
         out_words = out_1[0].rearrange("p n r -> p (n r)").bitcast(I32)
-        left_second = keep.tile([P, 4, HALF], F32, name="left_second")
-        right = [keep.tile([P, 4, HALF], F32, name="right%d" % a) for a in range(2)]
+        right_first = keep.tile([P, 4, HALF], F32, name="right_first")
         res = [keep.tile([P, 4, HALF], F32, name="res%d" % a) for a in range(2)]
         rounded = [keep.tile([P, HALF, 4], BF16, name="rounded%d" % a, align_bytes=64) for a in range(2)]
 
         def left_product(dst, a, t, plain):
             nc.vector.tensor_tensor(dst, d[t][:].indirect(half_list(n3_sb, a)), plain, MULT)
 
-        def right_product(a, t):
-            nc.vector.tensor_tensor(right[a][:, t, :], h[t][:].indirect(half_list(n2_sb, a)), d[t][:, half_cols(a)], MULT)
+        def right_product(dst, a, t):
+            nc.vector.tensor_tensor(dst, h[t][:].indirect(half_list(n2_sb, a)), d[t][:, half_cols(a)], MULT)
 
         def quantise_result(a):
             codes = keep.tile([P, HALF], I32, name="codes%d" % a, align_bytes=64)
@@ -206,45 +216,46 @@ def tile_picked_latecrossbbig_none_po_kernel(
         for t in range(3):
             left_product(left_early[:, t, :], 0, t, h_neg[t][:])
         h_products(1)
-        left_late = keep.tile([P, HALF], F32, name="left_late", tag="woven1", align_bytes=64)
-        left_product(left_late[:], 0, 3, h_neg[3][:])
-        left_first = [left_early[:, 0, :], left_early[:, 1, :], left_early[:, 2, :], left_late[:]]
+        left_late = keep.tile([P, 2, HALF], F32, name="left_late", tag="planes1", align_bytes=64)
+        left_product(left_late[:, 0, :], 0, 3, h_neg[3][:])
+        nc.vector.tensor_copy(left_late[:, 1, :], d[0][:].indirect(half_list(n3_sb, 1)))
+        left_first = [left_early[:, 0, :], left_early[:, 1, :], left_early[:, 2, :], left_late[:, 0, :]]
         for t in range(4):
             nc.scalar.activation(h[t][:], h_acc[t][:], COPY)
-        for pair in range(2):
-            turned = bank(4 + pair)
-            for u in range(2):
-                t = 2 * pair + u
-                right_product(0, t)
+        for g, (lo, hi) in enumerate(ROW_GROUPS):
+            width = (hi - lo) * HALF
+            turned = bank(4 + g)
+            for t in range(lo, hi):
+                right_product(right_first[:, t, :], 0, t)
                 for b in range(2):
                     blk = slice(P * b, P * (b + 1))
-                    dst = turned[:, HALF * u + P * b : HALF * u + P * (b + 1)]
+                    dst = turned[:, HALF * (t - lo) + P * b : HALF * (t - lo) + P * (b + 1)]
                     nc.tensor.matmul(dst, left_first[t][:, blk], ident[:], start=True, stop=False, is_transpose=True)
-                    nc.tensor.matmul(dst, right[0][:, t, blk], ident[:], start=False, stop=True, is_transpose=True)
-            turned_sb = keep.tile([P, S], F32, name="turned_sb%d" % pair)
-            nc.scalar.activation(turned_sb[:], turned[:], COPY, scale=-1.0)
-            back = bank(6 + pair)
-            for b in range(4):
+                    nc.tensor.matmul(dst, right_first[:, t, blk], ident[:], start=False, stop=True, is_transpose=True)
+            turned_sb = keep.tile([P, width], F32, name="turned_sb%d" % g)
+            nc.scalar.activation(turned_sb[:], turned[:, :width], COPY, scale=-1.0)
+            back = bank(g)
+            for b in range(width // P):
                 blk = slice(P * b, P * (b + 1))
                 nc.tensor.transpose(back[:, blk], turned_sb[:, blk], ident[:])
-            rows = slice(2 * pair, 2 * pair + 2)
-            nc.scalar.activation(res[0][:, rows, :].rearrange("p t j -> p (t j)"), back[:], COPY)
-            nc.sync.dma_start(out_rows[:, rows, half_cols(0)], res[0][:, rows, :])
-        nc.scalar.copy(rounded[0][:], res[0][:].rearrange("p t j -> p j t"))
+            nc.scalar.activation(res[0][:, lo:hi, :].rearrange("p t j -> p (t j)"), back[:, :width], COPY)
+            nc.sync.dma_start(out_rows[:, lo:hi, half_cols(0)], res[0][:, lo:hi, :])
+        weave(nc.scalar.copy, rounded[0][:], res[0][:])
 
+        second = keep.tile([P, 2, 4, HALF], F32, name="second", tag="left_early")
+        nc.vector.tensor_tensor(second[:, 0, 0, :], left_late[:, 1, :], h[0][:, half_cols(1)], MULT)
+        for t in range(1, 4):
+            left_product(second[:, 0, t, :], 1, t, h[t][:, half_cols(1)])
         for t in range(4):
-            left_product(left_second[:, t, :], 1, t, h[t][:, half_cols(1)])
-        for t in range(4):
-            right_product(1, t)
-            if t == 1:
-                quantise_result(0)
-        for lo, hi in [(0, 2), (2, 3), (3, 4)]:
-            nc.vector.tensor_tensor(res[1][:, lo:hi, :], left_second[:, lo:hi, :], right[1][:, lo:hi, :], SUB)
-            nc.sync.dma_start(out_rows[:, lo:hi, half_cols(1)], res[1][:, lo:hi, :])
-        by_col = res[1][:].rearrange("p t j -> p j t")
-        nc.scalar.copy(rounded[1][:, V_COLS:, :], by_col[:, V_COLS:, :])
-        nc.vector.tensor_copy(rounded[1][:, :V_COLS, :], by_col[:, :V_COLS, :])
-        quantise_result(1)
+            right_product(second[:, 1, t, :], 1, t)
+        for lo, hi in ROW_GROUPS:
+            nc.vector.tensor_tensor(res[1][:, lo:hi, :], second[:, 0, lo:hi, :], second[:, 1, lo:hi, :], SUB)
+            if hi % 2 == 0:
+                nc.sync.dma_start(out_rows[:, hi - 2 : hi, half_cols(1)], res[1][:, hi - 2 : hi, :])
+        weave(nc.scalar.copy, rounded[1][:, V_COLS:, :], res[1][:, :, V_COLS:])
+        weave(nc.vector.tensor_copy, rounded[1][:, :V_COLS, :], res[1][:, :, :V_COLS])
+        for a in range(2):
+            quantise_result(a)
         for q in range(4):
             queue = nc.scalar if q % 2 == 0 else nc.sync
             queue.dma_start(

@@ -19,8 +19,9 @@ P = 128
 T = 2048
 S = 512
 HALF = S // 2
+W2_SCALE_START = 4
 ROW_GROUPS = ((0, 2), (2, 3), (3, 4))
-V_COLS = 176
+VECTOR_COLUMNS = 144
 FLOPS = 3 * 2 * 512 * 512 * 512
 
 
@@ -43,15 +44,12 @@ def tile_picked_latecrossbbig_none_po_kernel(
             nc.sync.dma_start(tile[:], src[0].rearrange("p n r -> p (n r)").bitcast(I32))
             return tile
 
-        def load_scale_rows(tile, src, first):
-            for q in range(4):
-                nc.sync.dma_start(
-                    tile[32 * q + first : 32 * q + first + 4, :].bitcast(I32),
-                    src[0, 4 * q : 4 * q + 4, :].bitcast(I32),
-                )
+        def load_scale_rows(tile, src, start):
+            for r in range(4):
+                nc.sync.dma_start(tile[start + r : P : 32, :].bitcast(I32), src[0, r:16:4, :].bitcast(I32))
 
-        def deal(name, raw, dtype, tag=""):
-            dealt = keep.tile([P, S], dtype, name=name, tag=tag or name, align_bytes=64)
+        def deal(name, raw, dtype):
+            dealt = keep.tile([P, S], dtype, name=name, align_bytes=64)
             run = 4 if dtype == I32 else P
             nc.vector.tensor_copy(
                 dealt[:].rearrange("p (t c i) -> p c t i", t=4, i=run),
@@ -78,15 +76,15 @@ def tile_picked_latecrossbbig_none_po_kernel(
         ident = keep.tile([P, P], F32, name="ident")
         make_identity(nc, ident[:])
 
+        w1_raw = load_words("w1_raw", w1_words, S)
         offs_sb = load_list("offs_sb", offs)
         load_scale_rows(xs, x_scales, 0)
         two_sb = load_list("two_sb", two)
         xw = load_words("xw", x_words, T)
         load_scale_rows(ws1_raw, w1_scales, 0)
-        w1_raw = load_words("w1_raw", w1_words, S)
         w3_raw = load_words("w3_raw", w3_words, S)
         load_scale_rows(ws32_raw, w3_scales, 0)
-        load_scale_rows(ws32_raw, w2_scales, 4)
+        load_scale_rows(ws32_raw, w2_scales, W2_SCALE_START)
         n1_sb = load_list("n1_sb", n1)
         gn_sb = keep.tile([P, 4], F32, name="gn_sb")
         nc.sync.dma_start(gn_sb[:], gn.rearrange("(p t) o -> p (t o)", t=4))
@@ -107,18 +105,18 @@ def tile_picked_latecrossbbig_none_po_kernel(
         def bank(index):
             return psum.tile([P, S], F32, name="acc", tag="bank%d" % index)
 
-        def product(acc, words, scales, first, t, rhs_words, rhs_scales):
+        def product(acc, words, scales, scale_start, t, rhs_words, rhs_scales):
             cols = slice(P * t, P * (t + 1))
             nc.tensor.matmul_mx(
-                out=acc, lhsT=words[:, cols].bitcast(FP8X4), lhsT_scale=scales[first:P, cols],
+                out=acc, lhsT=words[:, cols].bitcast(FP8X4), lhsT_scale=scales[scale_start:P, cols],
                 rhs=rhs_words[:].bitcast(FP8X4), rhs_scale=rhs_scales[:], start=True, stop=True,
             )
 
+        w1 = deal("w1", w1_raw, I32)
         xs_one = pick_scales("xs_one", offs_sb)
         xs_two = pick_scales("xs_two", two_sb)
         xw_one = pick_words("xw_one", offs_sb, "xw_one")
         ws1 = deal("ws1", ws1_raw, U8)
-        w1 = deal("w1", w1_raw, I32)
 
         y = []
         for t in range(4):
@@ -129,66 +127,71 @@ def tile_picked_latecrossbbig_none_po_kernel(
             y.append(y_t)
 
         w3 = deal("w3", w3_raw, I32)
-        xw_two = pick_words("xw_two", two_sb, "w1_raw")
+        xw_two = pick_words("xw_two", two_sb, "ws1_raw")
         ws32 = deal("ws32", ws32_raw, U8)
 
-        planes = [keep.tile([P, 4, HALF], BF16, name="planes%d" % a, tag="planes%d" % a, align_bytes=64) for a in range(2)]
-        woven = [keep.tile([P, HALF, 4], BF16, name="woven%d" % a, align_bytes=64) for a in range(2)]
+        z_rows = [
+            keep.tile([P, 4, HALF], BF16, name="z_rows%d" % a, tag="z_rows%d" % a, align_bytes=64) for a in range(2)
+        ]
+        z_woven = [keep.tile([P, HALF, 4], BF16, name="z_woven%d" % a, align_bytes=64) for a in range(2)]
         larger = [keep.tile([P, 4, HALF], F32, name="larger%d" % a) for a in range(2)]
         d = [keep.tile([P, S], F32, name="d%d" % t) for t in range(4)]
         h = [keep.tile([P, S], F32, name="h%d" % t) for t in range(4)]
         h_neg = [keep.tile([P, HALF], F32, name="h_neg%d" % t) for t in range(4)]
 
-        def fetch(dst, t, a):
+        def fetch_y(dst, t, a):
             nc.vector.tensor_copy(dst, y[t][:].indirect(half_list(n1_sb, a)))
 
-        def larger_scaled(fetched, t, a):
+        def make_z(fetched, t, a):
             nc.vector.tensor_tensor(larger[a][:, t, :], fetched, y[t][:, half_cols(a)], MAX)
-            nc.scalar.activation(planes[a][:, t, :], larger[a][:, t, :], COPY, scale=gn_sb[:, t : t + 1])
+            nc.scalar.activation(z_rows[a][:, t, :], larger[a][:, t, :], COPY, scale=gn_sb[:, t : t + 1])
 
         def weave_z(a):
-            weave(nc.scalar.copy, woven[a][:], planes[a][:])
+            weave(nc.scalar.copy, z_woven[a][:], z_rows[a][:])
 
         def h_products(a):
             zw = keep.tile([P, HALF], U32, name="zw%d" % a, align_bytes=64)
             zs = keep.tile([P, HALF], U8, name="zs%d" % a, align_bytes=64)
-            nc.vector.quantize_mx(out=zw[:].bitcast(FP8X4), scales=zs[:], in_=woven[a][:].rearrange("p j t -> p (j t)"))
+            nc.vector.quantize_mx(
+                out=zw[:].bitcast(FP8X4), scales=zs[:], in_=z_woven[a][:].rearrange("p j t -> p (j t)")
+            )
             for t in range(4):
-                product(h_acc[t][:, half_cols(a)], w2, ws32, 4, t, zw, zs)
+                product(h_acc[t][:, half_cols(a)], w2, ws32, W2_SCALE_START, t, zw, zs)
 
         def d_product(t):
             acc = bank(4 + t)
             product(acc[:], w3, ws32, 0, t, xw_two, xs_two)
             nc.scalar.activation(d[t][:], acc[:], COPY, scale=0.75)
 
-        def negated_h(t):
+        def negate_h(t):
             nc.scalar.activation(h_neg[t][:], h_acc[t][:, half_cols(0)], COPY, scale=-1.0)
 
         for t in range(3):
             d_product(t)
         yn_first = keep.tile([P, 4, HALF], F32, name="yn_first")
         for t in range(4):
-            fetch(yn_first[:, t, :], t, 0)
+            fetch_y(yn_first[:, t, :], t, 0)
         for t in range(4):
-            larger_scaled(yn_first[:, t, :], t, 0)
+            make_z(yn_first[:, t, :], t, 0)
         d_product(3)
         weave_z(0)
+
         yn_early = keep.tile([P, 2, HALF], F32, name="yn_early")
         for t in range(2):
-            fetch(yn_early[:, t, :], t, 1)
+            fetch_y(yn_early[:, t, :], t, 1)
         for t in range(2):
-            larger_scaled(yn_early[:, t, :], t, 1)
+            make_z(yn_early[:, t, :], t, 1)
         w2 = deal("w2", w2_raw, I32)
         h_acc = [bank(t) for t in range(4)]
         h_products(0)
         for t in range(3):
-            negated_h(t)
-        yn_late = keep.tile([P, 2, HALF], F32, name="yn_late", tag="planes0", align_bytes=64)
+            negate_h(t)
+        yn_late = keep.tile([P, 2, HALF], F32, name="yn_late", tag="z_rows0", align_bytes=64)
         for t in range(2, 4):
-            fetch(yn_late[:, t - 2, :], t, 1)
+            fetch_y(yn_late[:, t - 2, :], t, 1)
         for t in range(2, 4):
-            larger_scaled(yn_late[:, t - 2, :], t, 1)
-        negated_h(3)
+            make_z(yn_late[:, t - 2, :], t, 1)
+        negate_h(3)
         weave_z(1)
 
         out_scales = keep.tile([P, S], U8, name="out_scales", align_bytes=64)
@@ -216,46 +219,74 @@ def tile_picked_latecrossbbig_none_po_kernel(
         for t in range(3):
             left_product(left_early[:, t, :], 0, t, h_neg[t][:])
         h_products(1)
-        left_late = keep.tile([P, 2, HALF], F32, name="left_late", tag="planes1", align_bytes=64)
+        left_late = keep.tile([P, 2, HALF], F32, name="left_late", tag="z_rows1", align_bytes=64)
         left_product(left_late[:, 0, :], 0, 3, h_neg[3][:])
-        nc.vector.tensor_copy(left_late[:, 1, :], d[0][:].indirect(half_list(n3_sb, 1)))
+        d_fetched = left_late[:, 1, :]
+        nc.vector.tensor_copy(d_fetched, d[0][:].indirect(half_list(n3_sb, 1)))
         left_first = [left_early[:, 0, :], left_early[:, 1, :], left_early[:, 2, :], left_late[:, 0, :]]
         for t in range(4):
             nc.scalar.activation(h[t][:], h_acc[t][:], COPY)
-        for g, (lo, hi) in enumerate(ROW_GROUPS):
+
+        def difference_by_transposes(a, lo, hi, neg_lefts, rights, turned_bank, back_bank):
             width = (hi - lo) * HALF
-            turned = bank(4 + g)
+            turned = bank(turned_bank)
             for t in range(lo, hi):
-                right_product(right_first[:, t, :], 0, t)
-                for b in range(2):
+                for b in range(HALF // P):
                     blk = slice(P * b, P * (b + 1))
                     dst = turned[:, HALF * (t - lo) + P * b : HALF * (t - lo) + P * (b + 1)]
-                    nc.tensor.matmul(dst, left_first[t][:, blk], ident[:], start=True, stop=False, is_transpose=True)
-                    nc.tensor.matmul(dst, right_first[:, t, blk], ident[:], start=False, stop=True, is_transpose=True)
-            turned_sb = keep.tile([P, width], F32, name="turned_sb%d" % g)
+                    nc.tensor.matmul(dst, neg_lefts[t][:, blk], ident[:], start=True, stop=False, is_transpose=True)
+                    nc.tensor.matmul(dst, rights[t][:, blk], ident[:], start=False, stop=True, is_transpose=True)
+            turned_sb = keep.tile([P, width], F32, name="turned_sb%d_%d" % (a, lo))
             nc.scalar.activation(turned_sb[:], turned[:, :width], COPY, scale=-1.0)
-            back = bank(g)
+            back = bank(back_bank)
             for b in range(width // P):
                 blk = slice(P * b, P * (b + 1))
                 nc.tensor.transpose(back[:, blk], turned_sb[:, blk], ident[:])
-            nc.scalar.activation(res[0][:, lo:hi, :].rearrange("p t j -> p (t j)"), back[:, :width], COPY)
+            nc.scalar.activation(res[a][:, lo:hi, :].rearrange("p t j -> p (t j)"), back[:, :width], COPY)
+
+        h_neg_second = keep.tile([P, HALF], F32, name="h_neg_second")
+        nc.scalar.activation(h_neg_second[:], h_acc[0][:, half_cols(1)], COPY, scale=-1.0)
+        rights_first = [right_first[:, t, :] for t in range(4)]
+        for g, (lo, hi) in enumerate(ROW_GROUPS):
+            for t in range(lo, hi):
+                right_product(rights_first[t], 0, t)
+            difference_by_transposes(0, lo, hi, left_first, rights_first, 4 + g, g)
             nc.sync.dma_start(out_rows[:, lo:hi, half_cols(0)], res[0][:, lo:hi, :])
         weave(nc.scalar.copy, rounded[0][:], res[0][:])
 
         second = keep.tile([P, 2, 4, HALF], F32, name="second", tag="left_early")
-        nc.vector.tensor_tensor(second[:, 0, 0, :], left_late[:, 1, :], h[0][:, half_cols(1)], MULT)
-        for t in range(1, 4):
-            left_product(second[:, 0, t, :], 1, t, h[t][:, half_cols(1)])
-        for t in range(4):
-            right_product(second[:, 1, t, :], 1, t)
-        for lo, hi in ROW_GROUPS:
-            nc.vector.tensor_tensor(res[1][:, lo:hi, :], second[:, 0, lo:hi, :], second[:, 1, lo:hi, :], SUB)
-            if hi % 2 == 0:
-                nc.sync.dma_start(out_rows[:, hi - 2 : hi, half_cols(1)], res[1][:, hi - 2 : hi, :])
-        weave(nc.scalar.copy, rounded[1][:, V_COLS:, :], res[1][:, :, V_COLS:])
-        weave(nc.vector.tensor_copy, rounded[1][:, :V_COLS, :], res[1][:, :, :V_COLS])
+        lefts_second = [second[:, 0, t, :] for t in range(4)]
+        rights_second = [second[:, 1, t, :] for t in range(4)]
+
+        def left_second(t):
+            left_product(lefts_second[t], 1, t, h[t][:, half_cols(1)])
+
+        def right_second(t):
+            right_product(rights_second[t], 1, t)
+
+        def subtract(t):
+            nc.vector.tensor_tensor(res[1][:, t, :], lefts_second[t], rights_second[t], SUB)
+
+        nc.vector.tensor_tensor(lefts_second[0], d_fetched, h_neg_second[:], MULT)
+        right_second(0)
+        difference_by_transposes(1, 0, 1, lefts_second, rights_second, 7, 3)
+        nc.scalar.dma_start(out_rows[:, 0, half_cols(1)], res[1][:, 0, :])
+        left_second(1)
+        right_second(1)
+        left_second(2)
+        subtract(1)
+        nc.sync.dma_start(out_rows[:, 1, half_cols(1)], res[1][:, 1, :])
+        right_second(2)
+        left_second(3)
+        right_second(3)
+        subtract(2)
+        subtract(3)
+        nc.sync.dma_start(out_rows[:, 2:4, half_cols(1)], res[1][:, 2:4, :])
+        weave(nc.scalar.copy, rounded[1][:, VECTOR_COLUMNS:, :], res[1][:, :, VECTOR_COLUMNS:])
+        weave(nc.vector.tensor_copy, rounded[1][:, :VECTOR_COLUMNS, :], res[1][:, :, :VECTOR_COLUMNS])
         for a in range(2):
             quantise_result(a)
+
         for q in range(4):
             queue = nc.scalar if q % 2 == 0 else nc.sync
             queue.dma_start(

from contextlib import ExitStack

import concourse.mybir as mybir
from concourse.masks import make_identity

F32 = mybir.dt.float32
BF16 = mybir.dt.bfloat16
I32 = mybir.dt.int32
U32 = mybir.dt.uint32
U16 = mybir.dt.uint16
U8 = mybir.dt.uint8
FP8X4 = mybir.dt.float8_e4m3fn_x4
COPY = mybir.ActivationFunctionType.Copy
MULT = mybir.AluOpType.mult
MAX = mybir.AluOpType.max
SUB = mybir.AluOpType.subtract

P = 128
T = 2048
S = 512
HALF = S // 2
W2_SCALE_START = 4
ROW_GROUPS = ((0, 2), (2, 3), (3, 4))
VECTOR_COLUMNS = 144
FLOPS = 3 * 2 * 512 * 512 * 512


def tile_picked_latecrossbbig_none_po_kernel(
    tc, x_words, x_scales, w1_words, w1_scales, gn, w2_words, w2_scales, w3_words, w3_scales,
    offs, n1, two, n2, n3, out_0, out_1, out_2,
):
    nc = tc.nc
    with ExitStack() as ctx:
        keep = ctx.enter_context(tc.tile_pool(name="keep", bufs=1))
        psum = ctx.enter_context(tc.psum_pool(name="psum", bufs=1))

        def load_list(name, src):
            tile = keep.tile([P, S // 16], U16, name=name)
            nc.sync.dma_start(tile[:], src)
            return tile

        def load_words(name, src, width):
            tile = keep.tile([P, width], I32, name=name, align_bytes=64)
            nc.sync.dma_start(tile[:], src[0].rearrange("p n r -> p (n r)").bitcast(I32))
            return tile

        def load_scale_rows(tile, src, start):
            for r in range(4):
                nc.sync.dma_start(tile[start + r : P : 32, :].bitcast(I32), src[0, r:16:4, :].bitcast(I32))

        def deal(name, raw, dtype):
            dealt = keep.tile([P, S], dtype, name=name, align_bytes=64)
            run = 4 if dtype == I32 else P
            nc.vector.tensor_copy(
                dealt[:].rearrange("p (t c i) -> p c t i", t=4, i=run),
                raw[:].rearrange("p (c i t) -> p c t i", t=4, i=run),
            )
            return dealt

        def weave(copy, dst, src):
            copy(dst.rearrange("p (c i) t -> p c t i", i=4), src.rearrange("p t (c i) -> p c t i", i=4))

        def half_cols(a):
            return slice(a * HALF, (a + 1) * HALF)

        def half_list(tile, a):
            return tile[:, a * (HALF // 16) : (a + 1) * (HALF // 16)]

        xs = keep.tile([P, T], U8, name="xs", align_bytes=64)
        nc.vector.memset(xs[:].bitcast(I32), 0)
        ws1_raw = keep.tile([P, S], U8, name="ws1_raw", align_bytes=64)
        ws32_raw = keep.tile([P, S], U8, name="ws32_raw", align_bytes=64)
        nc.vector.memset(ws1_raw[:].bitcast(I32), 0)
        nc.vector.memset(ws32_raw[:].bitcast(I32), 0)

        ident = keep.tile([P, P], F32, name="ident")
        make_identity(nc, ident[:])

        w1_raw = load_words("w1_raw", w1_words, S)
        offs_sb = load_list("offs_sb", offs)
        load_scale_rows(xs, x_scales, 0)
        two_sb = load_list("two_sb", two)
        xw = load_words("xw", x_words, T)
        load_scale_rows(ws1_raw, w1_scales, 0)
        w3_raw = load_words("w3_raw", w3_words, S)
        load_scale_rows(ws32_raw, w3_scales, 0)
        load_scale_rows(ws32_raw, w2_scales, W2_SCALE_START)
        n1_sb = load_list("n1_sb", n1)
        gn_sb = keep.tile([P, 4], F32, name="gn_sb")
        nc.sync.dma_start(gn_sb[:], gn.rearrange("(p t) o -> p (t o)", t=4))
        w2_raw = load_words("w2_raw", w2_words, S)
        n3_sb = load_list("n3_sb", n3)
        n2_sb = load_list("n2_sb", n2)

        def pick_scales(name, lst):
            tile = keep.tile([P, S], U8, name=name, align_bytes=64)
            nc.vector.tensor_copy(tile[:], xs[:].indirect(lst[:]))
            return tile

        def pick_words(name, lst, tag):
            tile = keep.tile([P, S], U32, name=name, tag=tag, align_bytes=64)
            nc.vector.tensor_copy(tile[:], xw[:].bitcast(U32).indirect(lst[:]))
            return tile

        def bank(index):
            return psum.tile([P, S], F32, name="acc", tag="bank%d" % index)

        def product(acc, words, scales, scale_start, t, rhs_words, rhs_scales):
            cols = slice(P * t, P * (t + 1))
            nc.tensor.matmul_mx(
                out=acc, lhsT=words[:, cols].bitcast(FP8X4), lhsT_scale=scales[scale_start:P, cols],
                rhs=rhs_words[:].bitcast(FP8X4), rhs_scale=rhs_scales[:], start=True, stop=True,
            )

        w1 = deal("w1", w1_raw, I32)
        xs_one = pick_scales("xs_one", offs_sb)
        xs_two = pick_scales("xs_two", two_sb)
        xw_one = pick_words("xw_one", offs_sb, "xw_one")
        ws1 = deal("ws1", ws1_raw, U8)

        y = []
        for t in range(4):
            acc = bank(t)
            product(acc[:], w1, ws1, 0, t, xw_one, xs_one)
            y_t = keep.tile([P, S], F32, name="y%d" % t)
            nc.scalar.activation(y_t[:], acc[:], COPY)
            y.append(y_t)

        w3 = deal("w3", w3_raw, I32)
        xw_two = pick_words("xw_two", two_sb, "ws1_raw")
        ws32 = deal("ws32", ws32_raw, U8)

        z_rows = [
            keep.tile([P, 4, HALF], BF16, name="z_rows%d" % a, tag="z_rows%d" % a, align_bytes=64) for a in range(2)
        ]
        z_woven = [keep.tile([P, HALF, 4], BF16, name="z_woven%d" % a, align_bytes=64) for a in range(2)]
        larger = [keep.tile([P, 4, HALF], F32, name="larger%d" % a) for a in range(2)]
        d = [keep.tile([P, S], F32, name="d%d" % t) for t in range(4)]
        h = [keep.tile([P, S], F32, name="h%d" % t) for t in range(4)]
        h_neg = [keep.tile([P, HALF], F32, name="h_neg%d" % t) for t in range(4)]

        def fetch_y(dst, t, a):
            nc.vector.tensor_copy(dst, y[t][:].indirect(half_list(n1_sb, a)))

        def make_z(fetched, t, a):
            nc.vector.tensor_tensor(larger[a][:, t, :], fetched, y[t][:, half_cols(a)], MAX)
            nc.scalar.activation(z_rows[a][:, t, :], larger[a][:, t, :], COPY, scale=gn_sb[:, t : t + 1])

        def weave_z(a):
            weave(nc.scalar.copy, z_woven[a][:], z_rows[a][:])

        def h_products(a):
            zw = keep.tile([P, HALF], U32, name="zw%d" % a, align_bytes=64)
            zs = keep.tile([P, HALF], U8, name="zs%d" % a, align_bytes=64)
            nc.vector.quantize_mx(
                out=zw[:].bitcast(FP8X4), scales=zs[:], in_=z_woven[a][:].rearrange("p j t -> p (j t)")
            )
            for t in range(4):
                product(h_acc[t][:, half_cols(a)], w2, ws32, W2_SCALE_START, t, zw, zs)

        def d_product(t):
            acc = bank(4 + t)
            product(acc[:], w3, ws32, 0, t, xw_two, xs_two)
            nc.scalar.activation(d[t][:], acc[:], COPY, scale=0.75)

        def negate_h(t):
            nc.scalar.activation(h_neg[t][:], h_acc[t][:, half_cols(0)], COPY, scale=-1.0)

        for t in range(3):
            d_product(t)
        yn_first = keep.tile([P, 4, HALF], F32, name="yn_first")
        for t in range(4):
            fetch_y(yn_first[:, t, :], t, 0)
        for t in range(4):
            make_z(yn_first[:, t, :], t, 0)
        d_product(3)
        weave_z(0)

        yn_early = keep.tile([P, 2, HALF], F32, name="yn_early")
        for t in range(2):
            fetch_y(yn_early[:, t, :], t, 1)
        for t in range(2):
            make_z(yn_early[:, t, :], t, 1)
        w2 = deal("w2", w2_raw, I32)
        h_acc = [bank(t) for t in range(4)]
        h_products(0)
        for t in range(3):
            negate_h(t)
        yn_late = keep.tile([P, 2, HALF], F32, name="yn_late", tag="z_rows0", align_bytes=64)
        for t in range(2, 4):
            fetch_y(yn_late[:, t - 2, :], t, 1)
        for t in range(2, 4):
            make_z(yn_late[:, t - 2, :], t, 1)
        negate_h(3)
        weave_z(1)

        out_scales = keep.tile([P, S], U8, name="out_scales", align_bytes=64)
        out_rows = out_0.rearrange("(p t) j -> p t j", t=4)
        out_words = out_1[0].rearrange("p n r -> p (n r)").bitcast(I32)
        right_first = keep.tile([P, 4, HALF], F32, name="right_first")
        res = [keep.tile([P, 4, HALF], F32, name="res%d" % a) for a in range(2)]
        rounded = [keep.tile([P, HALF, 4], BF16, name="rounded%d" % a, align_bytes=64) for a in range(2)]

        def left_product(dst, a, t, plain):
            nc.vector.tensor_tensor(dst, d[t][:].indirect(half_list(n3_sb, a)), plain, MULT)

        def right_product(dst, a, t):
            nc.vector.tensor_tensor(dst, h[t][:].indirect(half_list(n2_sb, a)), d[t][:, half_cols(a)], MULT)

        def quantise_result(a):
            codes = keep.tile([P, HALF], I32, name="codes%d" % a, align_bytes=64)
            nc.vector.quantize_mx(
                out=codes[:].bitcast(FP8X4), scales=out_scales[:, half_cols(a)],
                in_=rounded[a][:].rearrange("p j t -> p (j t)"),
            )
            nc.sync.dma_start(out_words[:, half_cols(a)], codes[:])

        left_early = keep.tile([P, 3, HALF], F32, name="left_early")
        for t in range(3):
            left_product(left_early[:, t, :], 0, t, h_neg[t][:])
        h_products(1)
        left_late = keep.tile([P, 2, HALF], F32, name="left_late", tag="z_rows1", align_bytes=64)
        left_product(left_late[:, 0, :], 0, 3, h_neg[3][:])
        d_fetched = left_late[:, 1, :]
        nc.vector.tensor_copy(d_fetched, d[0][:].indirect(half_list(n3_sb, 1)))
        left_first = [left_early[:, 0, :], left_early[:, 1, :], left_early[:, 2, :], left_late[:, 0, :]]
        for t in range(4):
            nc.scalar.activation(h[t][:], h_acc[t][:], COPY)

        def difference_by_transposes(a, lo, hi, neg_lefts, rights, turned_bank, back_bank):
            width = (hi - lo) * HALF
            turned = bank(turned_bank)
            for t in range(lo, hi):
                for b in range(HALF // P):
                    blk = slice(P * b, P * (b + 1))
                    dst = turned[:, HALF * (t - lo) + P * b : HALF * (t - lo) + P * (b + 1)]
                    nc.tensor.matmul(dst, neg_lefts[t][:, blk], ident[:], start=True, stop=False, is_transpose=True)
                    nc.tensor.matmul(dst, rights[t][:, blk], ident[:], start=False, stop=True, is_transpose=True)
            turned_sb = keep.tile([P, width], F32, name="turned_sb%d_%d" % (a, lo))
            nc.scalar.activation(turned_sb[:], turned[:, :width], COPY, scale=-1.0)
            back = bank(back_bank)
            for b in range(width // P):
                blk = slice(P * b, P * (b + 1))
                nc.tensor.transpose(back[:, blk], turned_sb[:, blk], ident[:])
            nc.scalar.activation(res[a][:, lo:hi, :].rearrange("p t j -> p (t j)"), back[:, :width], COPY)

        h_neg_second = keep.tile([P, HALF], F32, name="h_neg_second")
        nc.scalar.activation(h_neg_second[:], h_acc[0][:, half_cols(1)], COPY, scale=-1.0)
        rights_first = [right_first[:, t, :] for t in range(4)]
        for g, (lo, hi) in enumerate(ROW_GROUPS):
            for t in range(lo, hi):
                right_product(rights_first[t], 0, t)
            difference_by_transposes(0, lo, hi, left_first, rights_first, 4 + g, g)
            nc.sync.dma_start(out_rows[:, lo:hi, half_cols(0)], res[0][:, lo:hi, :])
        weave(nc.scalar.copy, rounded[0][:], res[0][:])

        second = keep.tile([P, 2, 4, HALF], F32, name="second", tag="left_early")
        lefts_second = [second[:, 0, t, :] for t in range(4)]
        rights_second = [second[:, 1, t, :] for t in range(4)]

        def left_second(t):
            left_product(lefts_second[t], 1, t, h[t][:, half_cols(1)])

        def right_second(t):
            right_product(rights_second[t], 1, t)

        def subtract(t):
            nc.vector.tensor_tensor(res[1][:, t, :], lefts_second[t], rights_second[t], SUB)

        nc.vector.tensor_tensor(lefts_second[0], d_fetched, h_neg_second[:], MULT)
        right_second(0)
        difference_by_transposes(1, 0, 1, lefts_second, rights_second, 7, 3)
        nc.scalar.dma_start(out_rows[:, 0, half_cols(1)], res[1][:, 0, :])
        left_second(1)
        right_second(1)
        left_second(2)
        subtract(1)
        nc.sync.dma_start(out_rows[:, 1, half_cols(1)], res[1][:, 1, :])
        right_second(2)
        left_second(3)
        right_second(3)
        subtract(2)
        subtract(3)
        nc.sync.dma_start(out_rows[:, 2:4, half_cols(1)], res[1][:, 2:4, :])
        weave(nc.scalar.copy, rounded[1][:, VECTOR_COLUMNS:, :], res[1][:, :, VECTOR_COLUMNS:])
        weave(nc.vector.tensor_copy, rounded[1][:, :VECTOR_COLUMNS, :], res[1][:, :, :VECTOR_COLUMNS])
        for a in range(2):
            quantise_result(a)

        for q in range(4):
            queue = nc.scalar if q % 2 == 0 else nc.sync
            queue.dma_start(
                out_2[0, 4 * q : 4 * q + 4, :].bitcast(I32), out_scales[32 * q : 32 * q + 4, :].bitcast(I32)
            )
